import numpy as np
import ml_dtypes

BF16 = ml_dtypes.bfloat16


def bf(x):
    return np.asarray(x, np.float32).astype(BF16)


def f32(x):
    return np.asarray(x, np.float32)


def f64(x):
    return np.asarray(x).astype(np.float64)


def striped(idx):
    return np.tile(idx.reshape(-1, 16).T, (8, 1))


S, K, M, N, E, Q = 256, 128, 128, 128, 2, 64


def gelu_tanh(v):
    return 0.5 * v * (1.0 + np.tanh(np.sqrt(2.0 / np.pi) * (v + 0.044715 * v**3)))


def setup_inputs():
    return {"base": bf(np.random.standard_normal((M, S))), "x": bf(np.random.standard_normal((K, N))), "w": bf(np.random.standard_normal((E, K, M)) / np.sqrt(K)), "b": f32(0.5 * np.random.standard_normal((M, 1))), "offs": striped(np.random.permutation(S)[:N])}


def reference(base, x, w, b, offs):
    idx = offs[:16].T.reshape(-1)
    z = f64(base).copy()
    for e in range(E):
        z[:, idx[e * Q : (e + 1) * Q]] += f64(w)[e].T @ f64(x)[:, e * Q : (e + 1) * Q]
    return gelu_tanh(z + f64(b))

@@ -1,0 +1,49 @@
+import concourse.mybir as mybir
+from concourse.masks import make_identity
+
+S, K, M, N, E = 256, 128, 128, 128, 2
+Q = N // E
+COLS = Q // 16
+FLOPS = 2 * K * M * N
+
+BF16 = mybir.dt.bfloat16
+F32 = mybir.dt.float32
+U16 = mybir.dt.uint16
+GELU = mybir.ActivationFunctionType.Gelu_apprx_tanh
+
+
+def tile_scatter_matmul_kernel(tc, base, x, w, b, offs, out):
+    nc = tc.nc
+    with (
+        tc.tile_pool(name="held", bufs=1) as held,
+        tc.psum_pool(name="psum", bufs=1) as psum,
+    ):
+        offsets = held.tile([128, N // 16], U16, name="offsets")
+        nc.sync.dma_start(offsets[:], offs)
+        residual = held.tile([M, S], BF16, name="residual")
+        nc.sync.dma_start(residual[:], base)
+        tokens = held.tile([K, N], BF16, name="tokens")
+        nc.sync.dma_start(tokens[:], x)
+        weights = held.tile([K, E, M], BF16, name="weights")
+        nc.scalar.dma_start(weights[:], w.rearrange("e k m -> k e m"))
+        bias = held.tile([M, 1], F32, name="bias")
+        nc.scalar.dma_start(bias[:], b)
+
+        identity = held.tile([M, M], BF16, name="identity")
+        make_identity(nc, identity[:])
+
+        window = psum.tile([M, S], F32, name="window")
+        nc.tensor.matmul(window[:], identity[:], residual[:], start=True, stop=False)
+
+        for e in range(E):
+            nc.tensor.matmul(
+                window[:].indirect(offsets[:, e * COLS : (e + 1) * COLS]),
+                weights[:, e, :],
+                tokens[:, e * Q : (e + 1) * Q],
+                start=False,
+                stop=(e == E - 1),
+            )
+
+        result = held.tile([M, S], F32, name="result")
+        nc.scalar.activation(result[:], window[:], GELU, bias=bias[:])
+        nc.sync.dma_start(out, result[:])

@@ -29,6 +29,10 @@ def tile_scatter_matmul_kernel(tc, base, x, w, b, offs, out):
         bias = held.tile([M, 1], F32, name="bias")
         nc.scalar.dma_start(bias[:], b)
 
+        warm = held.tile([M, 1], F32, name="warm")
+        nc.vector.memset(warm[:], 0.0)
+        nc.scalar.activation(warm[:], warm[:], GELU)
+
         identity = held.tile([M, M], BF16, name="identity")
         make_identity(nc, identity[:])
 

@@ -21,13 +21,13 @@ def tile_scatter_matmul_kernel(tc, base, x, w, b, offs, out):
         offsets = held.tile([128, N // 16], U16, name="offsets")
         nc.sync.dma_start(offsets[:], offs)
         residual = held.tile([M, S], BF16, name="residual")
-        nc.sync.dma_start(residual[:], base)
-        tokens = held.tile([K, N], BF16, name="tokens")
-        nc.sync.dma_start(tokens[:], x)
+        nc.scalar.dma_start(residual[:], base)
         weights = held.tile([K, E, M], BF16, name="weights")
-        nc.scalar.dma_start(weights[:], w.rearrange("e k m -> k e m"))
+        nc.sync.dma_start(weights[:], w.rearrange("e k m -> k e m"))
+        tokens = held.tile([K, N], BF16, name="tokens")
+        nc.scalar.dma_start(tokens[:], x)
         bias = held.tile([M, 1], F32, name="bias")
-        nc.scalar.dma_start(bias[:], b)
+        nc.sync.dma_start(bias[:], b)
 
         warm = held.tile([M, 1], F32, name="warm")
         nc.vector.memset(warm[:], 0.0)

@@ -18,14 +18,14 @@ def tile_scatter_matmul_kernel(tc, base, x, w, b, offs, out):
         tc.tile_pool(name="held", bufs=1) as held,
         tc.psum_pool(name="psum", bufs=1) as psum,
     ):
-        offsets = held.tile([128, N // 16], U16, name="offsets")
-        nc.sync.dma_start(offsets[:], offs)
         residual = held.tile([M, S], BF16, name="residual")
-        nc.scalar.dma_start(residual[:], base)
+        nc.sync.dma_start(residual[:], base)
         weights = held.tile([K, E, M], BF16, name="weights")
         nc.sync.dma_start(weights[:], w.rearrange("e k m -> k e m"))
         tokens = held.tile([K, N], BF16, name="tokens")
-        nc.scalar.dma_start(tokens[:], x)
+        nc.sync.dma_start(tokens[:], x)
+        offsets = held.tile([128, N // 16], U16, name="offsets")
+        nc.sync.dma_start(offsets[:], offs)
         bias = held.tile([M, 1], F32, name="bias")
         nc.sync.dma_start(bias[:], b)
 

@@ -4,6 +4,7 @@ from concourse.masks import make_identity
 S, K, M, N, E = 256, 128, 128, 128, 2
 Q = N // E
 COLS = Q // 16
+ROW_START = 256
 FLOPS = 2 * K * M * N
 
 BF16 = mybir.dt.bfloat16
@@ -18,15 +19,15 @@ def tile_scatter_matmul_kernel(tc, base, x, w, b, offs, out):
         tc.tile_pool(name="held", bufs=1) as held,
         tc.psum_pool(name="psum", bufs=1) as psum,
     ):
-        residual = held.tile([M, S], BF16, name="residual")
+        residual = held.tile([M, S], BF16, name="residual", align_bytes=ROW_START)
         nc.sync.dma_start(residual[:], base)
-        weights = held.tile([K, E, M], BF16, name="weights")
+        weights = held.tile([K, E, M], BF16, name="weights", align_bytes=ROW_START)
         nc.sync.dma_start(weights[:], w.rearrange("e k m -> k e m"))
-        tokens = held.tile([K, N], BF16, name="tokens")
+        tokens = held.tile([K, N], BF16, name="tokens", align_bytes=ROW_START)
         nc.sync.dma_start(tokens[:], x)
-        offsets = held.tile([128, N // 16], U16, name="offsets")
+        offsets = held.tile([128, N // 16], U16, name="offsets", align_bytes=ROW_START)
         nc.sync.dma_start(offsets[:], offs)
-        bias = held.tile([M, 1], F32, name="bias")
+        bias = held.tile([M, 1], F32, name="bias", align_bytes=ROW_START)
         nc.sync.dma_start(bias[:], b)
 
         warm = held.tile([M, 1], F32, name="warm")
@@ -48,6 +49,6 @@ def tile_scatter_matmul_kernel(tc, base, x, w, b, offs, out):
                 stop=(e == E - 1),
             )
 
-        result = held.tile([M, S], F32, name="result")
+        result = held.tile([M, S], F32, name="result", align_bytes=ROW_START)
         nc.scalar.activation(result[:], window[:], GELU, bias=bias[:])
         nc.sync.dma_start(out, result[:])

@@ -4,6 +4,10 @@ from concourse.masks import make_identity
 S, K, M, N, E = 256, 128, 128, 128, 2
 Q = N // E
 COLS = Q // 16
+BANK = 512
+STRIP = 32
+WARM_COLS = 256
+WARM_ROUNDS = 2
 ROW_START = 256
 FLOPS = 2 * K * M * N
 
@@ -30,9 +34,22 @@ def tile_scatter_matmul_kernel(tc, base, x, w, b, offs, out):
         bias = held.tile([M, 1], F32, name="bias", align_bytes=ROW_START)
         nc.sync.dma_start(bias[:], b)
 
-        warm = held.tile([M, 1], F32, name="warm")
-        nc.vector.memset(warm[:], 0.0)
-        nc.scalar.activation(warm[:], warm[:], GELU)
+        zeros = held.tile([K, WARM_COLS], BF16, name="zeros")
+        nc.vector.memset(zeros[:], 0.0)
+
+        spare = psum.tile([M, BANK], F32, name="spare")
+        for _ in range(WARM_ROUNDS):
+            for first in range(0, M, STRIP):
+                nc.tensor.matmul(
+                    spare[first : first + STRIP, 0:WARM_COLS],
+                    zeros[:, 0:STRIP],
+                    zeros[:],
+                    start=True,
+                    stop=True,
+                )
+
+        unused = held.tile([M, 1], F32, name="unused")
+        nc.scalar.activation(unused[:], zeros[:, 0:1], GELU)
 
         identity = held.tile([M, M], BF16, name="identity")
         make_identity(nc, identity[:])

@@ -25,12 +25,12 @@ def tile_scatter_matmul_kernel(tc, base, x, w, b, offs, out):
     ):
         residual = held.tile([M, S], BF16, name="residual", align_bytes=ROW_START)
         nc.sync.dma_start(residual[:], base)
+        offsets = held.tile([128, N // 16], U16, name="offsets", align_bytes=ROW_START)
+        nc.sync.dma_start(offsets[:], offs)
         weights = held.tile([K, E, M], BF16, name="weights", align_bytes=ROW_START)
         nc.sync.dma_start(weights[:], w.rearrange("e k m -> k e m"))
         tokens = held.tile([K, N], BF16, name="tokens", align_bytes=ROW_START)
         nc.sync.dma_start(tokens[:], x)
-        offsets = held.tile([128, N // 16], U16, name="offsets", align_bytes=ROW_START)
-        nc.sync.dma_start(offsets[:], offs)
         bias = held.tile([M, 1], F32, name="bias", align_bytes=ROW_START)
         nc.sync.dma_start(bias[:], b)
 

@@ -27,10 +27,13 @@ def tile_scatter_matmul_kernel(tc, base, x, w, b, offs, out):
         nc.sync.dma_start(residual[:], base)
         offsets = held.tile([128, N // 16], U16, name="offsets", align_bytes=ROW_START)
         nc.sync.dma_start(offsets[:], offs)
-        weights = held.tile([K, E, M], BF16, name="weights", align_bytes=ROW_START)
-        nc.sync.dma_start(weights[:], w.rearrange("e k m -> k e m"))
         tokens = held.tile([K, N], BF16, name="tokens", align_bytes=ROW_START)
         nc.sync.dma_start(tokens[:], x)
+        weights = []
+        for e in range(E):
+            expert_weights = held.tile([K, M], BF16, name=f"weights_{e}", align_bytes=ROW_START)
+            nc.sync.dma_start(expert_weights[:], w[e])
+            weights.append(expert_weights)
         bias = held.tile([M, 1], F32, name="bias", align_bytes=ROW_START)
         nc.sync.dma_start(bias[:], b)
 
@@ -60,7 +63,7 @@ def tile_scatter_matmul_kernel(tc, base, x, w, b, offs, out):
         for e in range(E):
             nc.tensor.matmul(
                 window[:].indirect(offsets[:, e * COLS : (e + 1) * COLS]),
-                weights[:, e, :],
+                weights[e][:],
                 tokens[:, e * Q : (e + 1) * Q],
                 start=False,
                 stop=(e == E - 1),

@@ -8,6 +8,7 @@ BANK = 512
 STRIP = 32
 WARM_COLS = 256
 WARM_ROUNDS = 2
+BLOCK = 32
 ROW_START = 256
 FLOPS = 2 * K * M * N
 
@@ -34,8 +35,9 @@ def tile_scatter_matmul_kernel(tc, base, x, w, b, offs, out):
             expert_weights = held.tile([K, M], BF16, name=f"weights_{e}", align_bytes=ROW_START)
             nc.sync.dma_start(expert_weights[:], w[e])
             weights.append(expert_weights)
-        bias = held.tile([M, 1], F32, name="bias", align_bytes=ROW_START)
-        nc.sync.dma_start(bias[:], b)
+        bias_rows = held.tile([M, BLOCK], F32, name="bias_rows", align_bytes=ROW_START)
+        nc.vector.memset(bias_rows[:], 0.0)
+        nc.sync.dma_start(bias_rows[0:M:BLOCK, :], b.rearrange("(q c) o -> q (c o)", c=BLOCK))
 
         zeros = held.tile([K, WARM_COLS], BF16, name="zeros")
         nc.vector.memset(zeros[:], 0.0)
@@ -54,6 +56,9 @@ def tile_scatter_matmul_kernel(tc, base, x, w, b, offs, out):
         unused = held.tile([M, 1], F32, name="unused")
         nc.scalar.activation(unused[:], zeros[:, 0:1], GELU)
 
+        bias = held.tile([M, BLOCK], F32, name="bias", align_bytes=ROW_START)
+        nc.vector.transpose(bias[:], bias_rows[:])
+
         identity = held.tile([M, M], BF16, name="identity")
         make_identity(nc, identity[:])
 
@@ -70,5 +75,5 @@ def tile_scatter_matmul_kernel(tc, base, x, w, b, offs, out):
             )
 
         result = held.tile([M, S], F32, name="result", align_bytes=ROW_START)
-        nc.scalar.activation(result[:], window[:], GELU, bias=bias[:])
+        nc.scalar.activation(result[:], window[:], GELU, bias=bias[:, 0:1])
         nc.sync.dma_start(out, result[:])

@@ -24,6 +24,9 @@ def tile_scatter_matmul_kernel(tc, base, x, w, b, offs, out):
         tc.tile_pool(name="held", bufs=1) as held,
         tc.psum_pool(name="psum", bufs=1) as psum,
     ):
+        zeros = held.tile([K, STRIP], BF16, name="zeros")
+        nc.vector.memset(zeros[:], 0.0)
+
         residual = held.tile([M, S], BF16, name="residual", align_bytes=ROW_START)
         nc.sync.dma_start(residual[:], base)
         offsets = held.tile([128, N // 16], U16, name="offsets", align_bytes=ROW_START)
@@ -39,16 +42,13 @@ def tile_scatter_matmul_kernel(tc, base, x, w, b, offs, out):
         nc.vector.memset(bias_rows[:], 0.0)
         nc.sync.dma_start(bias_rows[0:M:BLOCK, :], b.rearrange("(q c) o -> q (c o)", c=BLOCK))
 
-        zeros = held.tile([K, WARM_COLS], BF16, name="zeros")
-        nc.vector.memset(zeros[:], 0.0)
-
         spare = psum.tile([M, BANK], F32, name="spare")
         for _ in range(WARM_ROUNDS):
             for first in range(0, M, STRIP):
                 nc.tensor.matmul(
                     spare[first : first + STRIP, 0:WARM_COLS],
-                    zeros[:, 0:STRIP],
                     zeros[:],
+                    zeros[:, 0:1].to_broadcast([K, WARM_COLS]),
                     start=True,
                     stop=True,
                 )

@@ -27,17 +27,17 @@ def tile_scatter_matmul_kernel(tc, base, x, w, b, offs, out):
         zeros = held.tile([K, STRIP], BF16, name="zeros")
         nc.vector.memset(zeros[:], 0.0)
 
+        weights = [
+            held.tile([K, M], BF16, name=f"weights_{e}", align_bytes=ROW_START) for e in range(E)
+        ]
         residual = held.tile([M, S], BF16, name="residual", align_bytes=ROW_START)
         nc.sync.dma_start(residual[:], base)
+        nc.scalar.dma_start(weights[0][:], w[0])
         offsets = held.tile([128, N // 16], U16, name="offsets", align_bytes=ROW_START)
         nc.sync.dma_start(offsets[:], offs)
         tokens = held.tile([K, N], BF16, name="tokens", align_bytes=ROW_START)
-        nc.sync.dma_start(tokens[:], x)
-        weights = []
-        for e in range(E):
-            expert_weights = held.tile([K, M], BF16, name=f"weights_{e}", align_bytes=ROW_START)
-            nc.sync.dma_start(expert_weights[:], w[e])
-            weights.append(expert_weights)
+        nc.scalar.dma_start(tokens[:], x)
+        nc.sync.dma_start(weights[1][:], w[1])
         bias_rows = held.tile([M, BLOCK], F32, name="bias_rows", align_bytes=ROW_START)
         nc.vector.memset(bias_rows[:], 0.0)
         nc.sync.dma_start(bias_rows[0:M:BLOCK, :], b.rearrange("(q c) o -> q (c o)", c=BLOCK))

import concourse.mybir as mybir
from concourse.masks import make_identity

S, K, M, N, E = 256, 128, 128, 128, 2
Q = N // E
COLS = Q // 16
BANK = 512
STRIP = 32
WARM_COLS = 256
WARM_ROUNDS = 2
BLOCK = 32
ROW_START = 256
FLOPS = 2 * K * M * N

BF16 = mybir.dt.bfloat16
F32 = mybir.dt.float32
U16 = mybir.dt.uint16
GELU = mybir.ActivationFunctionType.Gelu_apprx_tanh


def tile_scatter_matmul_kernel(tc, base, x, w, b, offs, out):
    nc = tc.nc
    with (
        tc.tile_pool(name="held", bufs=1) as held,
        tc.psum_pool(name="psum", bufs=1) as psum,
    ):
        zeros = held.tile([K, STRIP], BF16, name="zeros")
        nc.vector.memset(zeros[:], 0.0)

        weights = [
            held.tile([K, M], BF16, name=f"weights_{e}", align_bytes=ROW_START) for e in range(E)
        ]
        residual = held.tile([M, S], BF16, name="residual", align_bytes=ROW_START)
        nc.sync.dma_start(residual[:], base)
        nc.scalar.dma_start(weights[0][:], w[0])
        offsets = held.tile([128, N // 16], U16, name="offsets", align_bytes=ROW_START)
        nc.sync.dma_start(offsets[:], offs)
        tokens = held.tile([K, N], BF16, name="tokens", align_bytes=ROW_START)
        nc.scalar.dma_start(tokens[:], x)
        nc.sync.dma_start(weights[1][:], w[1])
        bias_rows = held.tile([M, BLOCK], F32, name="bias_rows", align_bytes=ROW_START)
        nc.vector.memset(bias_rows[:], 0.0)
        nc.sync.dma_start(bias_rows[0:M:BLOCK, :], b.rearrange("(q c) o -> q (c o)", c=BLOCK))

        spare = psum.tile([M, BANK], F32, name="spare")
        for _ in range(WARM_ROUNDS):
            for first in range(0, M, STRIP):
                nc.tensor.matmul(
                    spare[first : first + STRIP, 0:WARM_COLS],
                    zeros[:],
                    zeros[:, 0:1].to_broadcast([K, WARM_COLS]),
                    start=True,
                    stop=True,
                )

        unused = held.tile([M, 1], F32, name="unused")
        nc.scalar.activation(unused[:], zeros[:, 0:1], GELU)

        bias = held.tile([M, BLOCK], F32, name="bias", align_bytes=ROW_START)
        nc.vector.transpose(bias[:], bias_rows[:])

        identity = held.tile([M, M], BF16, name="identity")
        make_identity(nc, identity[:])

        window = psum.tile([M, S], F32, name="window")
        nc.tensor.matmul(window[:], identity[:], residual[:], start=True, stop=False)

        for e in range(E):
            nc.tensor.matmul(
                window[:].indirect(offsets[:, e * COLS : (e + 1) * COLS]),
                weights[e][:],
                tokens[:, e * Q : (e + 1) * Q],
                start=False,
                stop=(e == E - 1),
            )

        result = held.tile([M, S], F32, name="result", align_bytes=ROW_START)
        nc.scalar.activation(result[:], window[:], GELU, bias=bias[:, 0:1])
        nc.sync.dma_start(out, result[:])
